import numpy as np
import ml_dtypes


def mxq(x, axis, fmt="e4m3"):
    dtype, down = {"e4m3": (ml_dtypes.float8_e4m3fn, 7), "e5m2": (ml_dtypes.float8_e5m2, 14)}[fmt]
    v = np.moveaxis(np.asarray(x, np.float32).astype(ml_dtypes.bfloat16).astype(np.float64), axis, -1)
    blocks = v.reshape(v.shape[:-1] + (-1, 32))
    amax = np.abs(blocks).max(-1, keepdims=True)
    byte = np.maximum(np.where(amax > 0, np.frexp(amax)[1] - 1 + 127, 0) - down, 1)
    scale = np.exp2(byte - 127.0)
    codes = (blocks / scale).astype(np.float32).astype(dtype).astype(np.float64)
    return np.moveaxis((codes * scale).reshape(v.shape), -1, axis)


WIDE = False


def mx_kscale(k):
    if not WIDE:
        return np.ones(k)
    levels = np.array([10, -10, 5, -5, 0])
    if k % 512:
        return np.exp2(np.random.permutation(np.resize(levels, k // 32))).repeat(32)
    a = np.empty((k // 512, 16))
    for p in range(k // 512):
        a[p, :8] = np.random.permutation(np.resize(levels, 8))
        for g in range(8):
            far = levels[np.abs(levels - a[p, g]) >= 10]
            a[p, g + 8] = far[np.random.randint(len(far))]
    return np.exp2(a.ravel()).repeat(32)


def f64(x):
    return np.asarray(x).astype(np.float64)


def striped8(idx):
    return np.asarray(idx).reshape(8, -1, 16).transpose(0, 2, 1).reshape(128, -1).astype(np.uint16)


def unstriped8(offs):
    return offs.reshape(8, 16, -1).transpose(0, 2, 1).reshape(8, -1).astype(np.int64)


def pick8(x, idx, run):
    r = np.arange(len(x))
    return x[r[:, None], idx[r % (8 * run) // run]]


E2M1 = np.array([0.0, 0.5, 1.0, 1.5, 2.0, 3.0, 4.0, 6.0, -0.0, -0.5, -1.0, -1.5, -2.0, -3.0, -4.0, -6.0])


def pack_weight(w, fmt):
    k, n = w.shape
    w = f64(np.asarray(w, np.float32).astype(ml_dtypes.bfloat16)).reshape(k // 32, 32, n)
    amax = np.abs(w).max(1)
    if fmt == "e4m3":
        byte = np.frexp(amax)[1] - 1 + 127 - 7
    else:
        mant, ex = np.frexp(amax / 6.0)
        byte = np.where(mant > 0.5, ex, ex - 1) + 127
    byte = np.clip(np.where(amax > 0, byte, 1), 1, 254)
    scaled = (w * np.exp2(127.0 - byte)[:, None, :]).reshape(k, n).astype(np.float32)
    by_word = np.ascontiguousarray(scaled.reshape(k // 512, 128, 4, n).transpose(0, 1, 3, 2))
    if fmt == "e4m3":
        words = by_word.astype(ml_dtypes.float8_e4m3fn).view(np.uint8)
    else:
        c = by_word.astype(ml_dtypes.float4_e2m1fn).view(np.uint8) & 0xF
        words = (c[..., 0::2] | (c[..., 1::2] << 4)).reshape(k // 512, 128, 2 * n)
    return np.ascontiguousarray(words), np.ascontiguousarray(byte.astype(np.uint8).reshape(k // 512, 16, n))


def unpack_weight(words, scales, fmt):
    g, _, n = scales.shape
    words = np.ascontiguousarray(words).reshape(g, 128, n, -1)
    if fmt == "e4m3":
        vals = words.view(ml_dtypes.float8_e4m3fn).astype(np.float64)
    else:
        nib = np.empty((g, 128, n, 4), np.uint8)
        nib[..., 0::2] = words & 0xF
        nib[..., 1::2] = words >> 4
        vals = E2M1[nib]
    vals = vals * np.repeat(np.exp2(scales.astype(np.float64) - 127.0), 8, axis=1)[..., None]
    return vals.transpose(0, 1, 3, 2).reshape(g * 512, n)


D, T, I, Q = 512, 1024, 512, 128


def setup_inputs():
    n = np.random.standard_normal
    idx = np.stack([np.random.permutation(T)[:I] for _ in range(8)])
    idx2 = np.stack([np.random.permutation(T)[:I] for _ in range(8)])
    idx3 = np.stack([np.random.permutation(T)[:I] for _ in range(8)])
    idx4 = np.stack([np.random.permutation(T)[:I] for _ in range(8)])
    fd = mx_kscale(D)
    keysp = pack_weight(n((D, T)) / fd[:, None], "e4m3")
    return {
        "query": (n((D, Q)) * 0.9 / np.sqrt(D) * fd[:, None]).astype(np.float32),
        "keys_words": keysp[0],
        "keys_scales": keysp[1],
        "lam": (np.random.uniform(0.7, 1.3, (Q, 1))).astype(np.float32),
        "reserve": (np.random.uniform(0.5, 2.0, (Q, 1))).astype(np.float32),
        "old": (np.random.uniform(0.0, 2.0, (Q, T))).astype(np.float32),
        "gainm": (np.random.uniform(0.5, 1.5, (Q, I))).astype(np.float32),
        "offs": striped8(idx),
        "offs2": striped8(idx2),
        "offs3": striped8(idx3),
        "offs4": striped8(idx4),
    }


def reference(query, keys_words, keys_scales, lam, reserve, old, gainm, offs, offs2, offs3, offs4):
    idx = unstriped8(offs)
    idx2 = unstriped8(offs2)
    idx3 = unstriped8(offs3)
    idx4 = unstriped8(offs4)
    keysu = unpack_weight(keys_words, keys_scales, "e4m3")
    queryq = mxq(f64(query), 0, "e4m3")
    a = queryq.T @ keysu
    s = pick8(a, idx, 16) * f64(lam) - np.abs(pick8(a, idx2, 16) - pick8(a, idx3, 16))
    p = np.exp(s - np.max(s, axis=1, keepdims=True))
    r = p / np.sum(p, axis=1, keepdims=True)
    u0 = r * np.log(r) * (-1.0)
    w = u0 / (np.sum(u0, axis=1, keepdims=True) + f64(reserve))
    ws = w * f64(gainm) * 512.0
    wf = np.zeros((Q, T))
    wf[np.arange(Q)[:, None], idx4[np.arange(Q) % 128 // 16]] = ws
    y = f64(old) + wf
    return y

@@ -1,0 +1,176 @@
+import math
+from contextlib import ExitStack
+
+import concourse.mybir as mybir
+
+D, T, I, Q = 512, 1024, 512, 128
+FLOPS = 2 * D * T * Q
+
+F32 = mybir.dt.float32
+BF16 = mybir.dt.bfloat16
+I32 = mybir.dt.int32
+U32 = mybir.dt.uint32
+U16 = mybir.dt.uint16
+U8 = mybir.dt.uint8
+FP8X4 = mybir.dt.float8_e4m3fn_x4
+ALU = mybir.AluOpType
+ACT = mybir.ActivationFunctionType
+AXIS = mybir.AxisListType
+
+P = 128
+PACK = 4
+LIST_COLS = I // 16
+N_PASS = 256
+HALF = I // 2
+TERMS = 30
+OUT_PIECE = 256
+EXPONENT_BITS = 0x7F800000
+SIGN_AND_EXPONENT_BITS = -0x00800000
+
+
+def tile_attend_betweentwo_lacking_moved_heads_kernel(
+    tc, query, keys_words, keys_scales, lam, reserve, old, gainm, offs, offs2, offs3, offs4, out
+):
+    nc = tc.nc
+    with ExitStack() as ctx:
+        sb = ctx.enter_context(tc.tile_pool(name="sb", bufs=1))
+        psum = ctx.enter_context(tc.psum_pool(name="psum", bufs=1))
+
+        k_scales = sb.tile([P, T], U8, name="k_scales", align_bytes=64)
+        nc.vector.memset(k_scales[:].bitcast(I32), 0)
+
+        q_raw = sb.tile([P, PACK, Q], F32, name="q_raw")
+        nc.sync.dma_start(out=q_raw[:], in_=query.rearrange("(p j) q -> p j q", j=PACK))
+        k_words = sb.tile([P, T], U32, name="k_words", align_bytes=64)
+        nc.sync.dma_start(
+            out=k_words[:].bitcast(I32), in_=keys_words[0].rearrange("p t r -> p (t r)").bitcast(I32)
+        )
+        for quad in range(4):
+            nc.sync.dma_start(
+                out=k_scales[32 * quad : 32 * quad + 4, :].bitcast(I32),
+                in_=keys_scales[0, 4 * quad : 4 * quad + 4, :].bitcast(I32),
+            )
+        list2 = sb.tile([P, LIST_COLS], U16, name="list2")
+        nc.sync.dma_start(list2[:], offs2)
+        list3 = sb.tile([P, LIST_COLS], U16, name="list3")
+        nc.sync.dma_start(list3[:], offs3)
+        list1 = sb.tile([P, LIST_COLS], U16, name="list1")
+        nc.sync.dma_start(list1[:], offs)
+        lam_t = sb.tile([P, 1], F32, name="lam_t")
+        nc.sync.dma_start(out=lam_t[:], in_=lam)
+        list4 = sb.tile([P, LIST_COLS], U16, name="list4")
+        nc.sync.dma_start(list4[:], offs4)
+        gain = sb.tile([P, I], F32, name="gain")
+        nc.sync.dma_start(out=gain[:], in_=gainm)
+        reserve_t = sb.tile([P, 1], F32, name="reserve_t")
+        nc.sync.dma_start(out=reserve_t[:], in_=reserve)
+        old_t = sb.tile([P, T], F32, name="old_t")
+        nc.sync.dma_start(out=old_t[:], in_=old)
+
+        minus_k = sb.tile([P, TERMS], F32, name="minus_k")
+        nc.gpsimd.iota(minus_k[:], [[1, TERMS]], base=-TERMS, channel_multiplier=0,
+                       allow_small_or_imprecise_dtypes=True)
+        quarter_powers = sb.tile([P, TERMS], F32, name="quarter_powers")
+        nc.scalar.activation(quarter_powers[:], minus_k[:], ACT.Exp, scale=math.log(4.0))
+        minus_inv_k = sb.tile([P, TERMS], F32, name="minus_inv_k")
+        nc.vector.reciprocal(minus_inv_k[:], minus_k[:])
+        series = sb.tile([P, TERMS + 1], F32, name="series")
+        nc.vector.tensor_tensor(series[:, 0:TERMS], quarter_powers[:], minus_inv_k[:], ALU.mult)
+
+        placed = sb.tile([P, T], F32, name="placed")
+        nc.vector.memset(placed[:], 0.0)
+
+        q_bf = sb.tile([P, Q, PACK], BF16, name="q_bf", align_bytes=64)
+        nc.vector.tensor_copy(out=q_bf[:], in_=q_raw[:].rearrange("p j q -> p q j"))
+        q_words = sb.tile([P, Q], U32, name="q_words", align_bytes=64)
+        q_scales = sb.tile([P, Q], U8, name="q_scales", align_bytes=64)
+        nc.vector.quantize_mx(
+            out=q_words[:].bitcast(FP8X4), scales=q_scales[:], in_=q_bf[:].rearrange("p q j -> p (q j)")
+        )
+
+        a = sb.tile([P, T], F32, name="a")
+        for n in range(T // N_PASS):
+            cols = slice(n * N_PASS, (n + 1) * N_PASS)
+            bank = psum.tile([P, N_PASS], F32, name="bank%d" % n)
+            nc.tensor.matmul_mx(
+                out=bank[:],
+                lhsT=q_words[:].bitcast(FP8X4),
+                lhsT_scale=q_scales[:],
+                rhs=k_words[:, cols].bitcast(FP8X4),
+                rhs_scale=k_scales[:, cols],
+                start=True,
+                stop=True,
+            )
+            if n % 2 == 0:
+                nc.scalar.copy(a[:, cols], bank[:])
+            else:
+                nc.vector.tensor_copy(a[:, cols], bank[:])
+
+        halves = [slice(h * HALF, (h + 1) * HALF) for h in range(2)]
+        list_halves = [slice(h * HALF // 16, (h + 1) * HALF // 16) for h in range(2)]
+        first = sb.tile([P, I], F32, name="first")
+        second = sb.tile([P, I], F32, name="second")
+        third = sb.tile([P, I], F32, name="third")
+        diff = sb.tile([P, I], F32, name="diff")
+        gap = sb.tile([P, I], F32, name="gap")
+        score = sb.tile([P, I + 1], F32, name="score")
+        for h in range(2):
+            nc.scalar.activation(second[:, halves[h]], a[:].indirect(list2[:, list_halves[h]]), ACT.Copy)
+        for h in range(2):
+            nc.vector.tensor_copy(third[:, halves[h]], a[:].indirect(list3[:, list_halves[h]]))
+        for h in range(2):
+            nc.scalar.activation(first[:, halves[h]], a[:].indirect(list1[:, list_halves[h]]), ACT.Copy)
+        for h in range(2):
+            nc.vector.tensor_tensor(diff[:, halves[h]], second[:, halves[h]], third[:, halves[h]], ALU.subtract)
+        for h in range(2):
+            nc.vector.scalar_tensor_tensor(
+                gap[:, halves[h]], diff[:, halves[h]], -1.0, diff[:, halves[h]], ALU.mult, ALU.max
+            )
+        for h in range(2):
+            nc.vector.scalar_tensor_tensor(
+                score[:, halves[h]], first[:, halves[h]], lam_t[:], gap[:, halves[h]], ALU.mult, ALU.subtract
+            )
+        minus_max = sb.tile([P, 1], F32, name="minus_max")
+        nc.vector.tensor_reduce(score[:, I : I + 1], score[:, halves[0]], AXIS.X, ALU.max)
+        nc.vector.tensor_reduce(minus_max[:], score[:, HALF : I + 1], AXIS.X, ALU.max, negate=True)
+
+        p = sb.tile([P, I], F32, name="p")
+        total = sb.tile([P, 1], F32, name="total")
+        nc.scalar.activation(p[:], score[:, 0:I], ACT.Exp, bias=minus_max[:], accum_out=total[:])
+        below_max = sb.tile([P, I], F32, name="below_max")
+        nc.vector.tensor_scalar(below_max[:], score[:, 0:I], minus_max[:], -1.0, ALU.add, ALU.mult)
+
+        power = sb.tile([P, 1], I32, name="power")
+        nc.vector.tensor_scalar(
+            power[:], total[:].bitcast(I32), EXPONENT_BITS, SIGN_AND_EXPONENT_BITS, ALU.bitwise_and, ALU.bitwise_xor
+        )
+        y = sb.tile([P, 1], F32, name="y")
+        nc.vector.tensor_scalar(y[:], total[:], power[:].bitcast(F32), 4.0, ALU.mult, ALU.add)
+        nc.vector.tensor_scalar(
+            series[:, TERMS : TERMS + 1], power[:], 127.0 * 2.0**23, -math.log(2.0) / 2.0**23, ALU.add, ALU.mult
+        )
+        horner = sb.tile([P, TERMS + 1], F32, name="horner")
+        nc.vector.tensor_tensor_scan(
+            horner[:], y[:].to_broadcast([P, TERMS + 1]), series[:], 0.0, ALU.mult, ALU.add
+        )
+        ln_total = horner[:, TERMS : TERMS + 1]
+
+        part = sb.tile([P, I], F32, name="part")
+        part_sum = sb.tile([P, 1], F32, name="part_sum")
+        nc.vector.scalar_tensor_tensor(
+            part[:], below_max[:], ln_total, p[:], ALU.add, ALU.mult, accum_out=part_sum[:]
+        )
+        nc.vector.tensor_tensor(placed[:].indirect(list4[:]), part[:], gain[:], ALU.mult)
+
+        divisor = sb.tile([P, 1], F32, name="divisor")
+        nc.scalar.activation(divisor[:], reserve_t[:], ACT.Identity, bias=part_sum[:], scale=total[:])
+        divisor512 = sb.tile([P, 1], F32, name="divisor512")
+        nc.scalar.activation(divisor512[:], divisor[:], ACT.Copy, scale=1.0 / 512.0)
+        factor = sb.tile([P, 1], F32, name="factor")
+        nc.vector.reciprocal(factor[:], divisor512[:])
+
+        for n in range(T // OUT_PIECE):
+            cols = slice(n * OUT_PIECE, (n + 1) * OUT_PIECE)
+            result = sb.tile([P, OUT_PIECE], F32, name="result%d" % n)
+            nc.vector.scalar_tensor_tensor(result[:], placed[:, cols], factor[:], old_t[:, cols], ALU.mult, ALU.add)
+            nc.sync.dma_start(out=out[:, cols], in_=result[:])

@@ -20,7 +20,7 @@ AXIS = mybir.AxisListType
 P = 128
 PACK = 4
 LIST_COLS = I // 16
-N_PASS = 256
+PASS_WIDTHS = (256, 256, 256, 128, 128)
 HALF = I // 2
 TERMS = 30
 OUT_PIECE = 256
@@ -41,15 +41,15 @@ def tile_attend_betweentwo_lacking_moved_heads_kernel(
 
         q_raw = sb.tile([P, PACK, Q], F32, name="q_raw")
         nc.sync.dma_start(out=q_raw[:], in_=query.rearrange("(p j) q -> p j q", j=PACK))
-        k_words = sb.tile([P, T], U32, name="k_words", align_bytes=64)
-        nc.sync.dma_start(
-            out=k_words[:].bitcast(I32), in_=keys_words[0].rearrange("p t r -> p (t r)").bitcast(I32)
-        )
+        words_hbm = keys_words[0].rearrange("p t r -> p (t r)").bitcast(I32)
+        k_words = [sb.tile([P, T // 2], U32, name="k_words%d" % u, align_bytes=64) for u in range(2)]
+        nc.sync.dma_start(out=k_words[0][:].bitcast(I32), in_=words_hbm[:, 0 : T // 2])
         for quad in range(4):
             nc.sync.dma_start(
                 out=k_scales[32 * quad : 32 * quad + 4, :].bitcast(I32),
                 in_=keys_scales[0, 4 * quad : 4 * quad + 4, :].bitcast(I32),
             )
+        nc.sync.dma_start(out=k_words[1][:].bitcast(I32), in_=words_hbm[:, T // 2 : T])
         list2 = sb.tile([P, LIST_COLS], U16, name="list2")
         nc.sync.dma_start(list2[:], offs2)
         list3 = sb.tile([P, LIST_COLS], U16, name="list3")
@@ -89,14 +89,17 @@ def tile_attend_betweentwo_lacking_moved_heads_kernel(
         )
 
         a = sb.tile([P, T], F32, name="a")
-        for n in range(T // N_PASS):
-            cols = slice(n * N_PASS, (n + 1) * N_PASS)
-            bank = psum.tile([P, N_PASS], F32, name="bank%d" % n)
+        start = 0
+        for n, width in enumerate(PASS_WIDTHS):
+            cols = slice(start, start + width)
+            words = k_words[start // (T // 2)][:, start % (T // 2) : start % (T // 2) + width]
+            start = start + width
+            bank = psum.tile([P, width], F32, name="bank%d" % n)
             nc.tensor.matmul_mx(
                 out=bank[:],
                 lhsT=q_words[:].bitcast(FP8X4),
                 lhsT_scale=q_scales[:],
-                rhs=k_words[:, cols].bitcast(FP8X4),
+                rhs=words.bitcast(FP8X4),
                 rhs_scale=k_scales[:, cols],
                 start=True,
                 stop=True,
@@ -113,7 +116,7 @@ def tile_attend_betweentwo_lacking_moved_heads_kernel(
         third = sb.tile([P, I], F32, name="third")
         diff = sb.tile([P, I], F32, name="diff")
         gap = sb.tile([P, I], F32, name="gap")
-        score = sb.tile([P, I + 1], F32, name="score")
+        score = sb.tile([P, I], F32, name="score")
         for h in range(2):
             nc.scalar.activation(second[:, halves[h]], a[:].indirect(list2[:, list_halves[h]]), ACT.Copy)
         for h in range(2):
@@ -131,14 +134,13 @@ def tile_attend_betweentwo_lacking_moved_heads_kernel(
                 score[:, halves[h]], first[:, halves[h]], lam_t[:], gap[:, halves[h]], ALU.mult, ALU.subtract
             )
         minus_max = sb.tile([P, 1], F32, name="minus_max")
-        nc.vector.tensor_reduce(score[:, I : I + 1], score[:, halves[0]], AXIS.X, ALU.max)
-        nc.vector.tensor_reduce(minus_max[:], score[:, HALF : I + 1], AXIS.X, ALU.max, negate=True)
+        nc.vector.tensor_reduce(minus_max[:], score[:], AXIS.X, ALU.max, negate=True)
 
         p = sb.tile([P, I], F32, name="p")
         total = sb.tile([P, 1], F32, name="total")
-        nc.scalar.activation(p[:], score[:, 0:I], ACT.Exp, bias=minus_max[:], accum_out=total[:])
+        nc.scalar.activation(p[:], score[:], ACT.Exp, bias=minus_max[:], accum_out=total[:])
         below_max = sb.tile([P, I], F32, name="below_max")
-        nc.vector.tensor_scalar(below_max[:], score[:, 0:I], minus_max[:], -1.0, ALU.add, ALU.mult)
+        nc.vector.tensor_scalar(below_max[:], score[:], minus_max[:], -1.0, ALU.add, ALU.mult)
 
         power = sb.tile([P, 1], I32, name="power")
         nc.vector.tensor_scalar(

@@ -23,6 +23,7 @@ LIST_COLS = I // 16
 PASS_WIDTHS = (256, 256, 256, 128, 128)
 HALF = I // 2
 TERMS = 30
+Q_ON_VECTOR = 84
 OUT_PIECE = 256
 EXPONENT_BITS = 0x7F800000
 SIGN_AND_EXPONENT_BITS = -0x00800000
@@ -70,18 +71,24 @@ def tile_attend_betweentwo_lacking_moved_heads_kernel(
         minus_k = sb.tile([P, TERMS], F32, name="minus_k")
         nc.gpsimd.iota(minus_k[:], [[1, TERMS]], base=-TERMS, channel_multiplier=0,
                        allow_small_or_imprecise_dtypes=True)
-        quarter_powers = sb.tile([P, TERMS], F32, name="quarter_powers")
-        nc.scalar.activation(quarter_powers[:], minus_k[:], ACT.Exp, scale=math.log(4.0))
-        minus_inv_k = sb.tile([P, TERMS], F32, name="minus_inv_k")
-        nc.vector.reciprocal(minus_inv_k[:], minus_k[:])
+        one_half = sb.tile([P, TERMS], F32, name="one_half")
+        nc.vector.memset(one_half[:], 0.5)
+        four_to_k = sb.tile([P, TERMS], F32, name="four_to_k")
+        nc.vector.tensor_tensor_scan(
+            four_to_k[:], one_half[:], one_half[:], 4.0 ** (TERMS + 1), ALU.mult, ALU.mult
+        )
+        series_divisors = sb.tile([P, TERMS], F32, name="series_divisors")
+        nc.vector.tensor_tensor(series_divisors[:], four_to_k[:], minus_k[:], ALU.mult)
         series = sb.tile([P, TERMS + 1], F32, name="series")
-        nc.vector.tensor_tensor(series[:, 0:TERMS], quarter_powers[:], minus_inv_k[:], ALU.mult)
+        nc.vector.reciprocal(series[:, 0:TERMS], series_divisors[:])
 
         placed = sb.tile([P, T], F32, name="placed")
         nc.vector.memset(placed[:], 0.0)
 
         q_bf = sb.tile([P, Q, PACK], BF16, name="q_bf", align_bytes=64)
-        nc.vector.tensor_copy(out=q_bf[:], in_=q_raw[:].rearrange("p j q -> p q j"))
+        q_by_row = q_raw[:].rearrange("p j q -> p q j")
+        nc.vector.tensor_copy(out=q_bf[:, 0:Q_ON_VECTOR, :], in_=q_by_row[:, 0:Q_ON_VECTOR, :])
+        nc.scalar.activation(q_bf[:, Q_ON_VECTOR:Q, :], q_by_row[:, Q_ON_VECTOR:Q, :], ACT.Copy)
         q_words = sb.tile([P, Q], U32, name="q_words", align_bytes=64)
         q_scales = sb.tile([P, Q], U8, name="q_scales", align_bytes=64)
         nc.vector.quantize_mx(

import math
from contextlib import ExitStack

import concourse.mybir as mybir

D, T, I, Q = 512, 1024, 512, 128
FLOPS = 2 * D * T * Q

F32 = mybir.dt.float32
BF16 = mybir.dt.bfloat16
I32 = mybir.dt.int32
U32 = mybir.dt.uint32
U16 = mybir.dt.uint16
U8 = mybir.dt.uint8
FP8X4 = mybir.dt.float8_e4m3fn_x4
ALU = mybir.AluOpType
ACT = mybir.ActivationFunctionType
AXIS = mybir.AxisListType

P = 128
PACK = 4
LIST_COLS = I // 16
PASS_WIDTHS = (256, 256, 256, 128, 128)
HALF = I // 2
TERMS = 30
Q_ON_VECTOR = 84
OUT_PIECE = 256
EXPONENT_BITS = 0x7F800000
SIGN_AND_EXPONENT_BITS = -0x00800000


def tile_attend_betweentwo_lacking_moved_heads_kernel(
    tc, query, keys_words, keys_scales, lam, reserve, old, gainm, offs, offs2, offs3, offs4, out
):
    nc = tc.nc
    with ExitStack() as ctx:
        sb = ctx.enter_context(tc.tile_pool(name="sb", bufs=1))
        psum = ctx.enter_context(tc.psum_pool(name="psum", bufs=1))

        k_scales = sb.tile([P, T], U8, name="k_scales", align_bytes=64)
        nc.vector.memset(k_scales[:].bitcast(I32), 0)

        q_raw = sb.tile([P, PACK, Q], F32, name="q_raw")
        nc.sync.dma_start(out=q_raw[:], in_=query.rearrange("(p j) q -> p j q", j=PACK))
        words_hbm = keys_words[0].rearrange("p t r -> p (t r)").bitcast(I32)
        k_words = [sb.tile([P, T // 2], U32, name="k_words%d" % u, align_bytes=64) for u in range(2)]
        nc.sync.dma_start(out=k_words[0][:].bitcast(I32), in_=words_hbm[:, 0 : T // 2])
        for quad in range(4):
            nc.sync.dma_start(
                out=k_scales[32 * quad : 32 * quad + 4, :].bitcast(I32),
                in_=keys_scales[0, 4 * quad : 4 * quad + 4, :].bitcast(I32),
            )
        nc.sync.dma_start(out=k_words[1][:].bitcast(I32), in_=words_hbm[:, T // 2 : T])
        list2 = sb.tile([P, LIST_COLS], U16, name="list2")
        nc.sync.dma_start(list2[:], offs2)
        list3 = sb.tile([P, LIST_COLS], U16, name="list3")
        nc.sync.dma_start(list3[:], offs3)
        list1 = sb.tile([P, LIST_COLS], U16, name="list1")
        nc.sync.dma_start(list1[:], offs)
        lam_t = sb.tile([P, 1], F32, name="lam_t")
        nc.sync.dma_start(out=lam_t[:], in_=lam)
        list4 = sb.tile([P, LIST_COLS], U16, name="list4")
        nc.sync.dma_start(list4[:], offs4)
        gain = sb.tile([P, I], F32, name="gain")
        nc.sync.dma_start(out=gain[:], in_=gainm)
        reserve_t = sb.tile([P, 1], F32, name="reserve_t")
        nc.sync.dma_start(out=reserve_t[:], in_=reserve)
        old_t = sb.tile([P, T], F32, name="old_t")
        nc.sync.dma_start(out=old_t[:], in_=old)

        minus_k = sb.tile([P, TERMS], F32, name="minus_k")
        nc.gpsimd.iota(minus_k[:], [[1, TERMS]], base=-TERMS, channel_multiplier=0,
                       allow_small_or_imprecise_dtypes=True)
        one_half = sb.tile([P, TERMS], F32, name="one_half")
        nc.vector.memset(one_half[:], 0.5)
        four_to_k = sb.tile([P, TERMS], F32, name="four_to_k")
        nc.vector.tensor_tensor_scan(
            four_to_k[:], one_half[:], one_half[:], 4.0 ** (TERMS + 1), ALU.mult, ALU.mult
        )
        series_divisors = sb.tile([P, TERMS], F32, name="series_divisors")
        nc.vector.tensor_tensor(series_divisors[:], four_to_k[:], minus_k[:], ALU.mult)
        series = sb.tile([P, TERMS + 1], F32, name="series")
        nc.vector.reciprocal(series[:, 0:TERMS], series_divisors[:])

        placed = sb.tile([P, T], F32, name="placed")
        nc.vector.memset(placed[:], 0.0)

        q_bf = sb.tile([P, Q, PACK], BF16, name="q_bf", align_bytes=64)
        q_by_row = q_raw[:].rearrange("p j q -> p q j")
        nc.vector.tensor_copy(out=q_bf[:, 0:Q_ON_VECTOR, :], in_=q_by_row[:, 0:Q_ON_VECTOR, :])
        nc.scalar.activation(q_bf[:, Q_ON_VECTOR:Q, :], q_by_row[:, Q_ON_VECTOR:Q, :], ACT.Copy)
        q_words = sb.tile([P, Q], U32, name="q_words", align_bytes=64)
        q_scales = sb.tile([P, Q], U8, name="q_scales", align_bytes=64)
        nc.vector.quantize_mx(
            out=q_words[:].bitcast(FP8X4), scales=q_scales[:], in_=q_bf[:].rearrange("p q j -> p (q j)")
        )

        a = sb.tile([P, T], F32, name="a")
        start = 0
        for n, width in enumerate(PASS_WIDTHS):
            cols = slice(start, start + width)
            words = k_words[start // (T // 2)][:, start % (T // 2) : start % (T // 2) + width]
            start = start + width
            bank = psum.tile([P, width], F32, name="bank%d" % n)
            nc.tensor.matmul_mx(
                out=bank[:],
                lhsT=q_words[:].bitcast(FP8X4),
                lhsT_scale=q_scales[:],
                rhs=words.bitcast(FP8X4),
                rhs_scale=k_scales[:, cols],
                start=True,
                stop=True,
            )
            if n % 2 == 0:
                nc.scalar.copy(a[:, cols], bank[:])
            else:
                nc.vector.tensor_copy(a[:, cols], bank[:])

        halves = [slice(h * HALF, (h + 1) * HALF) for h in range(2)]
        list_halves = [slice(h * HALF // 16, (h + 1) * HALF // 16) for h in range(2)]
        first = sb.tile([P, I], F32, name="first")
        second = sb.tile([P, I], F32, name="second")
        third = sb.tile([P, I], F32, name="third")
        diff = sb.tile([P, I], F32, name="diff")
        gap = sb.tile([P, I], F32, name="gap")
        score = sb.tile([P, I], F32, name="score")
        for h in range(2):
            nc.scalar.activation(second[:, halves[h]], a[:].indirect(list2[:, list_halves[h]]), ACT.Copy)
        for h in range(2):
            nc.vector.tensor_copy(third[:, halves[h]], a[:].indirect(list3[:, list_halves[h]]))
        for h in range(2):
            nc.scalar.activation(first[:, halves[h]], a[:].indirect(list1[:, list_halves[h]]), ACT.Copy)
        for h in range(2):
            nc.vector.tensor_tensor(diff[:, halves[h]], second[:, halves[h]], third[:, halves[h]], ALU.subtract)
        for h in range(2):
            nc.vector.scalar_tensor_tensor(
                gap[:, halves[h]], diff[:, halves[h]], -1.0, diff[:, halves[h]], ALU.mult, ALU.max
            )
        for h in range(2):
            nc.vector.scalar_tensor_tensor(
                score[:, halves[h]], first[:, halves[h]], lam_t[:], gap[:, halves[h]], ALU.mult, ALU.subtract
            )
        minus_max = sb.tile([P, 1], F32, name="minus_max")
        nc.vector.tensor_reduce(minus_max[:], score[:], AXIS.X, ALU.max, negate=True)

        p = sb.tile([P, I], F32, name="p")
        total = sb.tile([P, 1], F32, name="total")
        nc.scalar.activation(p[:], score[:], ACT.Exp, bias=minus_max[:], accum_out=total[:])
        below_max = sb.tile([P, I], F32, name="below_max")
        nc.vector.tensor_scalar(below_max[:], score[:], minus_max[:], -1.0, ALU.add, ALU.mult)

        power = sb.tile([P, 1], I32, name="power")
        nc.vector.tensor_scalar(
            power[:], total[:].bitcast(I32), EXPONENT_BITS, SIGN_AND_EXPONENT_BITS, ALU.bitwise_and, ALU.bitwise_xor
        )
        y = sb.tile([P, 1], F32, name="y")
        nc.vector.tensor_scalar(y[:], total[:], power[:].bitcast(F32), 4.0, ALU.mult, ALU.add)
        nc.vector.tensor_scalar(
            series[:, TERMS : TERMS + 1], power[:], 127.0 * 2.0**23, -math.log(2.0) / 2.0**23, ALU.add, ALU.mult
        )
        horner = sb.tile([P, TERMS + 1], F32, name="horner")
        nc.vector.tensor_tensor_scan(
            horner[:], y[:].to_broadcast([P, TERMS + 1]), series[:], 0.0, ALU.mult, ALU.add
        )
        ln_total = horner[:, TERMS : TERMS + 1]

        part = sb.tile([P, I], F32, name="part")
        part_sum = sb.tile([P, 1], F32, name="part_sum")
        nc.vector.scalar_tensor_tensor(
            part[:], below_max[:], ln_total, p[:], ALU.add, ALU.mult, accum_out=part_sum[:]
        )
        nc.vector.tensor_tensor(placed[:].indirect(list4[:]), part[:], gain[:], ALU.mult)

        divisor = sb.tile([P, 1], F32, name="divisor")
        nc.scalar.activation(divisor[:], reserve_t[:], ACT.Identity, bias=part_sum[:], scale=total[:])
        divisor512 = sb.tile([P, 1], F32, name="divisor512")
        nc.scalar.activation(divisor512[:], divisor[:], ACT.Copy, scale=1.0 / 512.0)
        factor = sb.tile([P, 1], F32, name="factor")
        nc.vector.reciprocal(factor[:], divisor512[:])

        for n in range(T // OUT_PIECE):
            cols = slice(n * OUT_PIECE, (n + 1) * OUT_PIECE)
            result = sb.tile([P, OUT_PIECE], F32, name="result%d" % n)
            nc.vector.scalar_tensor_tensor(result[:], placed[:, cols], factor[:], old_t[:, cols], ALU.mult, ALU.add)
            nc.sync.dma_start(out=out[:, cols], in_=result[:])
